import numpy as np
import ml_dtypes


def mxq(x, axis, fmt="e4m3"):
    dtype, down = {"e4m3": (ml_dtypes.float8_e4m3fn, 7), "e5m2": (ml_dtypes.float8_e5m2, 14)}[fmt]
    v = np.moveaxis(np.asarray(x, np.float32).astype(ml_dtypes.bfloat16).astype(np.float64), axis, -1)
    blocks = v.reshape(v.shape[:-1] + (-1, 32))
    amax = np.abs(blocks).max(-1, keepdims=True)
    byte = np.maximum(np.where(amax > 0, np.frexp(amax)[1] - 1 + 127, 0) - down, 1)
    scale = np.exp2(byte - 127.0)
    codes = (blocks / scale).astype(np.float32).astype(dtype).astype(np.float64)
    return np.moveaxis((codes * scale).reshape(v.shape), -1, axis)


WIDE = False


def mx_kscale(k):
    if not WIDE:
        return np.ones(k)
    levels = np.array([10, -10, 5, -5, 0])
    if k % 512:
        return np.exp2(np.random.permutation(np.resize(levels, k // 32))).repeat(32)
    a = np.empty((k // 512, 16))
    for p in range(k // 512):
        a[p, :8] = np.random.permutation(np.resize(levels, 8))
        for g in range(8):
            far = levels[np.abs(levels - a[p, g]) >= 10]
            a[p, g + 8] = far[np.random.randint(len(far))]
    return np.exp2(a.ravel()).repeat(32)


def f64(x):
    return np.asarray(x).astype(np.float64)


def striped(idx):
    return np.tile(idx.reshape(-1, 16).T, (8, 1)).astype(np.uint16)


def unstriped(offs):
    return offs[:16].T.reshape(-1).astype(np.int64)


def pack_weight(w):
    k, n = w.shape
    w = f64(np.asarray(w, np.float32).astype(ml_dtypes.bfloat16)).reshape(k // 32, 32, n)
    amax = np.abs(w).max(1)
    byte = np.clip(np.where(amax > 0, np.frexp(amax)[1] - 1 + 127 - 7, 1), 1, 254)
    scaled = (w * np.exp2(127.0 - byte)[:, None, :]).reshape(k, n).astype(np.float32)
    words = np.ascontiguousarray(scaled.reshape(k // 512, 128, 4, n).transpose(0, 1, 3, 2)).astype(ml_dtypes.float8_e4m3fn).view(np.uint8)
    return words, np.ascontiguousarray(byte.astype(np.uint8).reshape(k // 512, 16, n))


def unpack_weight(words, scales):
    g, p, n, _ = words.shape
    vals = np.ascontiguousarray(words).view(ml_dtypes.float8_e4m3fn).astype(np.float64) * np.repeat(np.exp2(scales.astype(np.float64) - 127.0), 8, axis=1)[..., None]
    return vals.transpose(0, 1, 3, 2).reshape(g * 512, n)


def silu(v):
    return v / (1.0 + np.exp(-np.maximum(v, -700.0)))


K, T, E, C, N = 512, 4096, 8, 256, 128


def by_expert(wq, xq):
    return np.concatenate([wq[e].T @ xq[:, e * C:(e + 1) * C] for e in range(E)], axis=1)


def setup_inputs():
    n = np.random.standard_normal
    s = mx_kscale(K)[:, None]
    packed = [pack_weight(m) for m in n((E, K, N)) / np.sqrt(K) / s[None]]
    return {
        "xT": (n((K, T)) * s).astype(np.float32),
        "xr": n((N, T)).astype(np.float32),
        "w_words": np.stack([m[0] for m in packed]),
        "w_scales": np.stack([m[1] for m in packed]),
        "b": (0.3 * n((N, E))).astype(np.float32),
        "gate": np.tile(np.random.uniform(0.2, 1.0, E * C), (N, 1)).astype(np.float32),
        "offs": striped(np.random.permutation(T)[:E * C]),
    }


def reference(xT, xr, w_words, w_scales, b, gate, offs):
    idx = unstriped(offs)
    w = np.stack([unpack_weight(w_words[e], w_scales[e]) for e in range(E)])
    xq = mxq(f64(xT)[:, idx], 0, "e4m3")
    y = by_expert(w, xq)
    y = silu(y + np.repeat(f64(b), C, axis=1))
    out = f64(xr).copy()
    out[:, idx] += f64(gate) * y
    return out

@@ -1,0 +1,115 @@
+from contextlib import ExitStack
+
+import concourse.mybir as mybir
+
+K, T, E, C, N = 512, 4096, 8, 256, 128
+SLOTS = E * C
+FLOPS = 2 * SLOTS * K * N
+
+F32 = mybir.dt.float32
+BF16 = mybir.dt.bfloat16
+U32 = mybir.dt.uint32
+I32 = mybir.dt.int32
+U16 = mybir.dt.uint16
+U8 = mybir.dt.uint8
+FP8X4 = mybir.dt.float8_e4m3fn_x4
+MULT = mybir.AluOpType.mult
+ADD = mybir.AluOpType.add
+SILU = mybir.ActivationFunctionType.Silu
+
+P = 128
+PACK = 4
+CHUNK = 512
+CHUNKS = SLOTS // CHUNK
+PER_CHUNK = CHUNK // C
+
+
+def tile_moe_res_lin_silu_kernel(tc, xT, xr, w_words, w_scales, b, gate, offs, out):
+    nc = tc.nc
+    with ExitStack() as ctx:
+        keep = ctx.enter_context(tc.tile_pool(name="keep", bufs=1))
+        psum = ctx.enter_context(tc.psum_pool(name="psum", bufs=1))
+
+        offsets = keep.tile([P, SLOTS // 16], U16, name="offsets")
+        planes = [keep.tile([P, T], F32, name=f"plane{t}") for t in range(PACK)]
+        w_codes = keep.tile([P, E, N], U32, name="w_codes", align_bytes=64)
+        w_bytes = keep.tile([P, E, N], U8, name="w_bytes", align_bytes=64)
+        bias = keep.tile([P, E], F32, name="bias")
+        weight = keep.tile([P, SLOTS], F32, name="weight")
+        picked = keep.tile([P, PACK, SLOTS], F32, name="picked", align_bytes=64)
+        grouped = keep.tile([P, SLOTS, PACK], BF16, name="grouped", align_bytes=64)
+        y = keep.tile([P, SLOTS], F32, name="y")
+        window = keep.tile([P, T], F32, name="window")
+        warm = keep.tile([P, 1], F32, name="warm")
+
+        nc.sync.dma_start(offsets[:], offs)
+        x_rows = xT.rearrange("(p t) w -> p t w", t=PACK)
+        for t in range(PACK):
+            nc.sync.dma_start(planes[t][:], x_rows[:, t, :])
+        nc.sync.dma_start(w_codes[:].bitcast(I32), w_words.rearrange("e a p n r -> p (e a) (n r)").bitcast(I32))
+        nc.sync.dma_start(weight[:], gate)
+
+        nc.vector.memset(w_bytes[:].bitcast(I32), 0)
+        nc.vector.memset(warm[:], 0.0)
+        nc.gpsimd.memset(window[:], 0.0)
+        s_rows = w_scales.rearrange("e a q n -> q (e a) n")
+        for q in range(4):
+            nc.scalar.dma_start(w_bytes[32 * q : 32 * q + 4, :, :].bitcast(I32), s_rows[4 * q : 4 * q + 4, :, :].bitcast(I32))
+        nc.scalar.dma_start(bias[:], b)
+        nc.scalar.activation(warm[:], warm[:], SILU)
+
+        xr_tiles = [keep.tile([P, T // 4], F32, name=f"xr{i}") for i in range(4)]
+        for i in range(4):
+            nc.sync.dma_start(xr_tiles[i][:], xr[:, i * (T // 4) : (i + 1) * (T // 4)])
+
+        def gather(t, first, last):
+            nc.vector.tensor_copy(picked[:, t, first:last], planes[t][:].indirect(offsets[:, first // 16 : last // 16]))
+
+        def interleave(t, first, last):
+            nc.scalar.copy(grouped[:, first:last, t : t + 2], picked[:, t : t + 2, first:last].rearrange("p t n -> p n t"))
+
+        for t in range(3):
+            for h in range(2):
+                gather(t, h * 1024, h * 1024 + 1024)
+                if t == 1:
+                    interleave(0, h * 1024, h * 1024 + 1024)
+        for c in range(CHUNKS):
+            gather(3, c * CHUNK, (c + 1) * CHUNK)
+            interleave(2, c * CHUNK, (c + 1) * CHUNK)
+
+        for c in range(CHUNKS):
+            codes = keep.tile([P, CHUNK], U32, name=f"codes{c}", align_bytes=64)
+            scales = keep.tile([P, CHUNK], U8, name=f"scales{c}", align_bytes=64)
+            nc.vector.quantize_mx(
+                out=codes[:].bitcast(FP8X4),
+                scales=scales[:],
+                in_=grouped[:, c * CHUNK : (c + 1) * CHUNK, :].rearrange("p n t -> p (n t)"),
+            )
+            acc = psum.tile([P, CHUNK], F32, name=f"acc{c}")
+            for i in range(PER_CHUNK):
+                e = c * PER_CHUNK + i
+                cols = slice(i * C, (i + 1) * C)
+                nc.tensor.matmul_mx(
+                    out=acc[:, cols],
+                    lhsT=w_codes[:, e, :].bitcast(FP8X4),
+                    lhsT_scale=w_bytes[:, e, :],
+                    rhs=codes[:, cols].bitcast(FP8X4),
+                    rhs_scale=scales[:, cols],
+                    start=True,
+                    stop=True,
+                )
+                nc.scalar.activation(y[:, e * C : (e + 1) * C], acc[:, cols], SILU, bias=bias[:, e : e + 1])
+            nc.vector.tensor_tensor(
+                window[:].indirect(offsets[:, c * (CHUNK // 16) : (c + 1) * (CHUNK // 16)]),
+                y[:, c * CHUNK : (c + 1) * CHUNK],
+                weight[:, c * CHUNK : (c + 1) * CHUNK],
+                MULT,
+            )
+
+        start = 0
+        for i, width in enumerate((512, 512, 1024, 1024, 512, 512)):
+            x = xr_tiles[start // 1024][:, start % 1024 : start % 1024 + width]
+            res = keep.tile([P, width], F32, name=f"res{i}")
+            nc.vector.tensor_tensor(res[:], window[:, start : start + width], x, ADD)
+            nc.sync.dma_start(out[:, start : start + width], res[:])
+            start += width

@@ -36,7 +36,9 @@ def tile_moe_res_lin_silu_kernel(tc, xT, xr, w_words, w_scales, b, gate, offs, o
         w_bytes = keep.tile([P, E, N], U8, name="w_bytes", align_bytes=64)
         bias = keep.tile([P, E], F32, name="bias")
         weight = keep.tile([P, SLOTS], F32, name="weight")
-        picked = keep.tile([P, PACK, SLOTS], F32, name="picked", align_bytes=64)
+        early = keep.tile([P, 2, SLOTS], F32, name="early", align_bytes=64)
+        shared = keep.tile([P, 3, CHUNK], F32, name="shared", align_bytes=64)
+        own = [keep.tile([P, 2, CHUNK], F32, name=f"own{i}", align_bytes=64) for i in range(2)]
         grouped = keep.tile([P, SLOTS, PACK], BF16, name="grouped", align_bytes=64)
         y = keep.tile([P, SLOTS], F32, name="y")
         window = keep.tile([P, T], F32, name="window")
@@ -58,39 +60,38 @@ def tile_moe_res_lin_silu_kernel(tc, xT, xr, w_words, w_scales, b, gate, offs, o
         nc.scalar.dma_start(bias[:], b)
         nc.scalar.activation(warm[:], warm[:], SILU)
 
-        xr_tiles = [keep.tile([P, T // 4], F32, name=f"xr{i}") for i in range(4)]
+        residual = keep.tile([P, T], F32, name="residual")
         for i in range(4):
-            nc.sync.dma_start(xr_tiles[i][:], xr[:, i * (T // 4) : (i + 1) * (T // 4)])
+            nc.sync.dma_start(residual[:, i * (T // 4) : (i + 1) * (T // 4)], xr[:, i * (T // 4) : (i + 1) * (T // 4)])
 
-        def gather(t, first, last):
-            nc.vector.tensor_copy(picked[:, t, first:last], planes[t][:].indirect(offsets[:, first // 16 : last // 16]))
+        late = [shared[:, 1:3, :], own[0][:], own[1][:], shared[:, 0:3:2, :]]
 
-        def interleave(t, first, last):
-            nc.scalar.copy(grouped[:, first:last, t : t + 2], picked[:, t : t + 2, first:last].rearrange("p t n -> p n t"))
+        def gather(t, first, last, into):
+            nc.vector.tensor_copy(into, planes[t][:].indirect(offsets[:, first // 16 : last // 16]))
 
-        for t in range(3):
-            for h in range(2):
-                gather(t, h * 1024, h * 1024 + 1024)
-                if t == 1:
-                    interleave(0, h * 1024, h * 1024 + 1024)
-        for c in range(CHUNKS):
-            gather(3, c * CHUNK, (c + 1) * CHUNK)
-            interleave(2, c * CHUNK, (c + 1) * CHUNK)
+        def late_gather(t, c):
+            gather(t, c * CHUNK, (c + 1) * CHUNK, late[c][:, t - 2, :])
 
-        for c in range(CHUNKS):
-            codes = keep.tile([P, CHUNK], U32, name=f"codes{c}", align_bytes=64)
-            scales = keep.tile([P, CHUNK], U8, name=f"scales{c}", align_bytes=64)
+        def interleave(t, first, last, pair):
+            nc.scalar.copy(grouped[:, first:last, t : t + 2], pair.rearrange("p t n -> p n t"))
+
+        def late_interleave(c):
+            interleave(2, c * CHUNK, (c + 1) * CHUNK, late[c])
+
+        banks = [psum.tile([P, C], F32, name=f"bank{e}") for e in range(E)]
+
+        def multiply(first, last):
+            codes = keep.tile([P, last - first], U32, name=f"codes{first}", align_bytes=64)
+            scales = keep.tile([P, last - first], U8, name=f"scales{first}", align_bytes=64)
             nc.vector.quantize_mx(
                 out=codes[:].bitcast(FP8X4),
                 scales=scales[:],
-                in_=grouped[:, c * CHUNK : (c + 1) * CHUNK, :].rearrange("p n t -> p (n t)"),
+                in_=grouped[:, first:last, :].rearrange("p n t -> p (n t)"),
             )
-            acc = psum.tile([P, CHUNK], F32, name=f"acc{c}")
-            for i in range(PER_CHUNK):
-                e = c * PER_CHUNK + i
-                cols = slice(i * C, (i + 1) * C)
+            for e in range(first // C, last // C):
+                cols = slice(e * C - first, e * C - first + C)
                 nc.tensor.matmul_mx(
-                    out=acc[:, cols],
+                    out=banks[e][:],
                     lhsT=w_codes[:, e, :].bitcast(FP8X4),
                     lhsT_scale=w_bytes[:, e, :],
                     rhs=codes[:, cols].bitcast(FP8X4),
@@ -98,17 +99,40 @@ def tile_moe_res_lin_silu_kernel(tc, xT, xr, w_words, w_scales, b, gate, offs, o
                     start=True,
                     stop=True,
                 )
-                nc.scalar.activation(y[:, e * C : (e + 1) * C], acc[:, cols], SILU, bias=bias[:, e : e + 1])
+                nc.scalar.activation(y[:, e * C : (e + 1) * C], banks[e][:], SILU, bias=bias[:, e : e + 1])
+
+        def scatter(first, last):
             nc.vector.tensor_tensor(
-                window[:].indirect(offsets[:, c * (CHUNK // 16) : (c + 1) * (CHUNK // 16)]),
-                y[:, c * CHUNK : (c + 1) * CHUNK],
-                weight[:, c * CHUNK : (c + 1) * CHUNK],
-                MULT,
+                window[:].indirect(offsets[:, first // 16 : last // 16]), y[:, first:last], weight[:, first:last], MULT
             )
 
+        gather(0, 0, SLOTS, early[:, 0, :])
+        for h in range(2):
+            half = slice(h * 1024, h * 1024 + 1024)
+            gather(1, half.start, half.stop, early[:, 1, half])
+            interleave(0, half.start, half.stop, early[:, :, half])
+        for c in range(CHUNKS):
+            late_gather(2, c)
+        late_gather(3, 0)
+        late_interleave(0)
+        late_gather(3, 1)
+        late_interleave(1)
+        late_gather(3, 2)
+        multiply(0, 512)
+        late_gather(3, 3)
+        multiply(512, 1024)
+        late_interleave(2)
+        scatter(0, 512)
+        multiply(1024, 1536)
+        late_interleave(3)
+        scatter(512, 1024)
+        multiply(1536, 2048)
+        scatter(1024, 1536)
+        scatter(1536, 2048)
+
         start = 0
-        for i, width in enumerate((512, 512, 1024, 1024, 512, 512)):
-            x = xr_tiles[start // 1024][:, start % 1024 : start % 1024 + width]
+        for i, width in enumerate((384, 896, 1024, 1024, 768)):
+            x = residual[:, start : start + width]
             res = keep.tile([P, width], F32, name=f"res{i}")
             nc.vector.tensor_tensor(res[:], window[:, start : start + width], x, ADD)
             nc.sync.dma_start(out[:, start : start + width], res[:])

@@ -38,12 +38,13 @@ def tile_moe_res_lin_silu_kernel(tc, xT, xr, w_words, w_scales, b, gate, offs, o
         weight = keep.tile([P, SLOTS], F32, name="weight")
         early = keep.tile([P, 2, SLOTS], F32, name="early", align_bytes=64)
         shared = keep.tile([P, 3, CHUNK], F32, name="shared", align_bytes=64)
-        own = [keep.tile([P, 2, CHUNK], F32, name=f"own{i}", align_bytes=64) for i in range(2)]
+        own = keep.tile([P, 2, 2 * CHUNK], F32, name="own", align_bytes=64)
         grouped = keep.tile([P, SLOTS, PACK], BF16, name="grouped", align_bytes=64)
         y = keep.tile([P, SLOTS], F32, name="y")
         window = keep.tile([P, T], F32, name="window")
         warm = keep.tile([P, 1], F32, name="warm")
 
+        nc.vector.memset(w_bytes[:].bitcast(I32), 0)
         nc.sync.dma_start(offsets[:], offs)
         x_rows = xT.rearrange("(p t) w -> p t w", t=PACK)
         for t in range(PACK):
@@ -51,20 +52,19 @@ def tile_moe_res_lin_silu_kernel(tc, xT, xr, w_words, w_scales, b, gate, offs, o
         nc.sync.dma_start(w_codes[:].bitcast(I32), w_words.rearrange("e a p n r -> p (e a) (n r)").bitcast(I32))
         nc.sync.dma_start(weight[:], gate)
 
-        nc.vector.memset(w_bytes[:].bitcast(I32), 0)
         nc.vector.memset(warm[:], 0.0)
-        nc.gpsimd.memset(window[:], 0.0)
         s_rows = w_scales.rearrange("e a q n -> q (e a) n")
         for q in range(4):
             nc.scalar.dma_start(w_bytes[32 * q : 32 * q + 4, :, :].bitcast(I32), s_rows[4 * q : 4 * q + 4, :, :].bitcast(I32))
         nc.scalar.dma_start(bias[:], b)
+        nc.gpsimd.memset(window[:], 0.0)
         nc.scalar.activation(warm[:], warm[:], SILU)
 
         residual = keep.tile([P, T], F32, name="residual")
         for i in range(4):
             nc.sync.dma_start(residual[:, i * (T // 4) : (i + 1) * (T // 4)], xr[:, i * (T // 4) : (i + 1) * (T // 4)])
 
-        late = [shared[:, 1:3, :], own[0][:], own[1][:], shared[:, 0:3:2, :]]
+        late = [shared[:, 1:3, :], own[:, :, 0:CHUNK], own[:, :, CHUNK : 2 * CHUNK], shared[:, 0:3:2, :]]
 
         def gather(t, first, last, into):
             nc.vector.tensor_copy(into, planes[t][:].indirect(offsets[:, first // 16 : last // 16]))
@@ -111,8 +111,9 @@ def tile_moe_res_lin_silu_kernel(tc, xT, xr, w_words, w_scales, b, gate, offs, o
             half = slice(h * 1024, h * 1024 + 1024)
             gather(1, half.start, half.stop, early[:, 1, half])
             interleave(0, half.start, half.stop, early[:, :, half])
-        for c in range(CHUNKS):
-            late_gather(2, c)
+        late_gather(2, 0)
+        gather(2, CHUNK, 3 * CHUNK, own[:, 0, :])
+        late_gather(2, 3)
         late_gather(3, 0)
         late_interleave(0)
         late_gather(3, 1)
@@ -131,7 +132,7 @@ def tile_moe_res_lin_silu_kernel(tc, xT, xr, w_words, w_scales, b, gate, offs, o
         scatter(1536, 2048)
 
         start = 0
-        for i, width in enumerate((384, 896, 1024, 1024, 768)):
+        for i, width in enumerate((256, 384, 512, 704, 896, 832, 512)):
             x = residual[:, start : start + width]
             res = keep.tile([P, width], F32, name=f"res{i}")
             nc.vector.tensor_tensor(res[:], window[:, start : start + width], x, ADD)

from contextlib import ExitStack

import concourse.mybir as mybir

K, T, E, C, N = 512, 4096, 8, 256, 128
SLOTS = E * C
FLOPS = 2 * SLOTS * K * N

F32 = mybir.dt.float32
BF16 = mybir.dt.bfloat16
U32 = mybir.dt.uint32
I32 = mybir.dt.int32
U16 = mybir.dt.uint16
U8 = mybir.dt.uint8
FP8X4 = mybir.dt.float8_e4m3fn_x4
MULT = mybir.AluOpType.mult
ADD = mybir.AluOpType.add
SILU = mybir.ActivationFunctionType.Silu

P = 128
PACK = 4
CHUNK = 512
CHUNKS = SLOTS // CHUNK
PER_CHUNK = CHUNK // C


def tile_moe_res_lin_silu_kernel(tc, xT, xr, w_words, w_scales, b, gate, offs, out):
    nc = tc.nc
    with ExitStack() as ctx:
        keep = ctx.enter_context(tc.tile_pool(name="keep", bufs=1))
        psum = ctx.enter_context(tc.psum_pool(name="psum", bufs=1))

        offsets = keep.tile([P, SLOTS // 16], U16, name="offsets")
        planes = [keep.tile([P, T], F32, name=f"plane{t}") for t in range(PACK)]
        w_codes = keep.tile([P, E, N], U32, name="w_codes", align_bytes=64)
        w_bytes = keep.tile([P, E, N], U8, name="w_bytes", align_bytes=64)
        bias = keep.tile([P, E], F32, name="bias")
        weight = keep.tile([P, SLOTS], F32, name="weight")
        early = keep.tile([P, 2, SLOTS], F32, name="early", align_bytes=64)
        shared = keep.tile([P, 3, CHUNK], F32, name="shared", align_bytes=64)
        own = keep.tile([P, 2, 2 * CHUNK], F32, name="own", align_bytes=64)
        grouped = keep.tile([P, SLOTS, PACK], BF16, name="grouped", align_bytes=64)
        y = keep.tile([P, SLOTS], F32, name="y")
        window = keep.tile([P, T], F32, name="window")
        warm = keep.tile([P, 1], F32, name="warm")

        nc.vector.memset(w_bytes[:].bitcast(I32), 0)
        nc.sync.dma_start(offsets[:], offs)
        x_rows = xT.rearrange("(p t) w -> p t w", t=PACK)
        for t in range(PACK):
            nc.sync.dma_start(planes[t][:], x_rows[:, t, :])
        nc.sync.dma_start(w_codes[:].bitcast(I32), w_words.rearrange("e a p n r -> p (e a) (n r)").bitcast(I32))
        nc.sync.dma_start(weight[:], gate)

        nc.vector.memset(warm[:], 0.0)
        s_rows = w_scales.rearrange("e a q n -> q (e a) n")
        for q in range(4):
            nc.scalar.dma_start(w_bytes[32 * q : 32 * q + 4, :, :].bitcast(I32), s_rows[4 * q : 4 * q + 4, :, :].bitcast(I32))
        nc.scalar.dma_start(bias[:], b)
        nc.gpsimd.memset(window[:], 0.0)
        nc.scalar.activation(warm[:], warm[:], SILU)

        residual = keep.tile([P, T], F32, name="residual")
        for i in range(4):
            nc.sync.dma_start(residual[:, i * (T // 4) : (i + 1) * (T // 4)], xr[:, i * (T // 4) : (i + 1) * (T // 4)])

        late = [shared[:, 1:3, :], own[:, :, 0:CHUNK], own[:, :, CHUNK : 2 * CHUNK], shared[:, 0:3:2, :]]

        def gather(t, first, last, into):
            nc.vector.tensor_copy(into, planes[t][:].indirect(offsets[:, first // 16 : last // 16]))

        def late_gather(t, c):
            gather(t, c * CHUNK, (c + 1) * CHUNK, late[c][:, t - 2, :])

        def interleave(t, first, last, pair):
            nc.scalar.copy(grouped[:, first:last, t : t + 2], pair.rearrange("p t n -> p n t"))

        def late_interleave(c):
            interleave(2, c * CHUNK, (c + 1) * CHUNK, late[c])

        banks = [psum.tile([P, C], F32, name=f"bank{e}") for e in range(E)]

        def multiply(first, last):
            codes = keep.tile([P, last - first], U32, name=f"codes{first}", align_bytes=64)
            scales = keep.tile([P, last - first], U8, name=f"scales{first}", align_bytes=64)
            nc.vector.quantize_mx(
                out=codes[:].bitcast(FP8X4),
                scales=scales[:],
                in_=grouped[:, first:last, :].rearrange("p n t -> p (n t)"),
            )
            for e in range(first // C, last // C):
                cols = slice(e * C - first, e * C - first + C)
                nc.tensor.matmul_mx(
                    out=banks[e][:],
                    lhsT=w_codes[:, e, :].bitcast(FP8X4),
                    lhsT_scale=w_bytes[:, e, :],
                    rhs=codes[:, cols].bitcast(FP8X4),
                    rhs_scale=scales[:, cols],
                    start=True,
                    stop=True,
                )
                nc.scalar.activation(y[:, e * C : (e + 1) * C], banks[e][:], SILU, bias=bias[:, e : e + 1])

        def scatter(first, last):
            nc.vector.tensor_tensor(
                window[:].indirect(offsets[:, first // 16 : last // 16]), y[:, first:last], weight[:, first:last], MULT
            )

        gather(0, 0, SLOTS, early[:, 0, :])
        for h in range(2):
            half = slice(h * 1024, h * 1024 + 1024)
            gather(1, half.start, half.stop, early[:, 1, half])
            interleave(0, half.start, half.stop, early[:, :, half])
        late_gather(2, 0)
        gather(2, CHUNK, 3 * CHUNK, own[:, 0, :])
        late_gather(2, 3)
        late_gather(3, 0)
        late_interleave(0)
        late_gather(3, 1)
        late_interleave(1)
        late_gather(3, 2)
        multiply(0, 512)
        late_gather(3, 3)
        multiply(512, 1024)
        late_interleave(2)
        scatter(0, 512)
        multiply(1024, 1536)
        late_interleave(3)
        scatter(512, 1024)
        multiply(1536, 2048)
        scatter(1024, 1536)
        scatter(1536, 2048)

        start = 0
        for i, width in enumerate((256, 384, 512, 704, 896, 832, 512)):
            x = residual[:, start : start + width]
            res = keep.tile([P, width], F32, name=f"res{i}")
            nc.vector.tensor_tensor(res[:], window[:, start : start + width], x, ADD)
            nc.sync.dma_start(out[:, start : start + width], res[:])
            start += width
